import numpy as np
import ml_dtypes


def mxq(x, axis, fmt="e4m3"):
    dtype, down = {"e4m3": (ml_dtypes.float8_e4m3fn, 7), "e5m2": (ml_dtypes.float8_e5m2, 14)}[fmt]
    v = np.moveaxis(np.asarray(x, np.float32).astype(ml_dtypes.bfloat16).astype(np.float64), axis, -1)
    blocks = v.reshape(v.shape[:-1] + (-1, 32))
    amax = np.abs(blocks).max(-1, keepdims=True)
    byte = np.maximum(np.where(amax > 0, np.frexp(amax)[1] - 1 + 127, 0) - down, 1)
    scale = np.exp2(byte - 127.0)
    codes = (blocks / scale).astype(np.float32).astype(dtype).astype(np.float64)
    return np.moveaxis((codes * scale).reshape(v.shape), -1, axis)


WIDE = False


def mx_kscale(k):
    if not WIDE:
        return np.ones(k)
    levels = np.array([10, -10, 5, -5, 0])
    if k % 512:
        return np.exp2(np.random.permutation(np.resize(levels, k // 32))).repeat(32)
    a = np.empty((k // 512, 16))
    for p in range(k // 512):
        a[p, :8] = np.random.permutation(np.resize(levels, 8))
        for g in range(8):
            far = levels[np.abs(levels - a[p, g]) >= 10]
            a[p, g + 8] = far[np.random.randint(len(far))]
    return np.exp2(a.ravel()).repeat(32)


def f64(x):
    return np.asarray(x).astype(np.float64)


def striped(idx):
    return np.tile(idx.reshape(-1, 16).T, (8, 1)).astype(np.uint16)


def unstriped(offs):
    return offs[:16].T.reshape(-1).astype(np.int64)


E2M1 = np.array([0.0, 0.5, 1.0, 1.5, 2.0, 3.0, 4.0, 6.0, -0.0, -0.5, -1.0, -1.5, -2.0, -3.0, -4.0, -6.0])


def pack_weight(w, fmt):
    k, n = w.shape
    w = f64(np.asarray(w, np.float32).astype(ml_dtypes.bfloat16)).reshape(k // 32, 32, n)
    amax = np.abs(w).max(1)
    if fmt == "e4m3":
        byte = np.frexp(amax)[1] - 1 + 127 - 7
    else:
        mant, ex = np.frexp(amax / 6.0)
        byte = np.where(mant > 0.5, ex, ex - 1) + 127
    byte = np.clip(np.where(amax > 0, byte, 1), 1, 254)
    scaled = (w * np.exp2(127.0 - byte)[:, None, :]).reshape(k, n).astype(np.float32)
    by_word = np.ascontiguousarray(scaled.reshape(k // 512, 128, 4, n).transpose(0, 1, 3, 2))
    if fmt == "e4m3":
        words = by_word.astype(ml_dtypes.float8_e4m3fn).view(np.uint8)
    else:
        c = by_word.astype(ml_dtypes.float4_e2m1fn).view(np.uint8) & 0xF
        words = (c[..., 0::2] | (c[..., 1::2] << 4)).reshape(k // 512, 128, 2 * n)
    return np.ascontiguousarray(words), np.ascontiguousarray(byte.astype(np.uint8).reshape(k // 512, 16, n))


def unpack_weight(words, scales, fmt):
    g, _, n = scales.shape
    words = np.ascontiguousarray(words).reshape(g, 128, n, -1)
    if fmt == "e4m3":
        vals = words.view(ml_dtypes.float8_e4m3fn).astype(np.float64)
    else:
        nib = np.empty((g, 128, n, 4), np.uint8)
        nib[..., 0::2] = words & 0xF
        nib[..., 1::2] = words >> 4
        vals = E2M1[nib]
    vals = vals * np.repeat(np.exp2(scales.astype(np.float64) - 127.0), 8, axis=1)[..., None]
    return vals.transpose(0, 1, 3, 2).reshape(g * 512, n)


def gelu(v):
    return 0.5 * v * (1.0 + np.tanh(np.sqrt(2.0 / np.pi) * (v + 0.044715 * v**3)))


K, H, T, S, T2, P = 1536, 1024, 2048, 512, 1024, 512

def setup_inputs():
    n = np.random.standard_normal
    s = mx_kscale(K)[:, None]
    u = mx_kscale(H)[:, None]
    d = {}
    d["tab_words"], d["tab_scales"] = pack_weight(n((K, T)) * s, "e4m3")
    d["offs"] = striped(np.random.permutation(T)[:S])
    d["offs2"] = striped(np.random.permutation(T2)[:S])
    d["offs3"] = striped(np.random.permutation(T2)[:P])
    d["w1"] = (1.6 * n((K, H)) / K ** 0.5 / s).astype(np.float32)
    d["w4_words"], d["w4_scales"] = pack_weight(n((K, H)) / K ** 0.5 / s, "e2m1")
    d["base"] = n((H, S)).astype(np.float32)
    d["gain"] = (0.8 * np.exp(0.3 * n(H)) * u[:, 0]).astype(np.float32)
    d["wgs"] = np.exp(0.3 * n((128, S))).astype(np.float32)
    d["page0"] = (n((H, T2)) * u).astype(np.float32)
    d["cap"] = (0.6 * np.exp(0.3 * n(H)) * u[:, 0]).astype(np.float32)
    d["wv"] = (2.5 * n(H) / H ** 0.5 / u[:, 0] ** 2).astype(np.float32)
    d["slot"] = (0.9 * np.exp(0.3 * n(T2))).astype(np.float32)
    return d

def reference(tab_words, tab_scales, offs, offs2, offs3, w1, w4_words, w4_scales, base, gain, wgs, page0, cap, wv, slot):
    v = unpack_weight(tab_words, tab_scales, "e4m3")[:, unstriped(offs)]
    first = mxq(f64(w1), 0, "e4m3").T @ v
    second = unpack_weight(w4_words, w4_scales, "e2m1").T @ v
    h = (np.tanh(first) + np.maximum(second, f64(base))) * f64(gain)[:, None]
    page = f64(page0).copy()
    page[:, unstriped(offs2)] = np.tile(f64(wgs), (H // 128, 1)) * h
    x = np.minimum(page[:, unstriped(offs3)], f64(cap)[:, None]) * f64(wv)[:, None]
    e = mxq(page, 0, "e4m3").T @ mxq(x, 0, "e4m3")
    return np.log(np.maximum(e, f64(slot)[:, None]))

@@ -1,0 +1,349 @@
+from contextlib import ExitStack
+
+import concourse.mybir as mybir
+
+K, H, T, S, T2, PJ = 1536, 1024, 2048, 512, 1024, 512
+FLOPS = 2 * (2 * K * H * S + H * T2 * PJ)
+
+F32 = mybir.dt.float32
+BF16 = mybir.dt.bfloat16
+I32 = mybir.dt.int32
+U32 = mybir.dt.uint32
+U16 = mybir.dt.uint16
+U8 = mybir.dt.uint8
+FP8X4 = mybir.dt.float8_e4m3fn_x4
+FP4X4 = mybir.dt.float4_e2m1fn_x4
+ALU = mybir.AluOpType
+ACT = mybir.ActivationFunctionType
+
+P = 128
+PACK = 4
+KP = P * PACK
+NA = K // KP
+NB = H // KP
+NS = NB * PACK
+NM = T2 // P
+W1_VECTOR_SHARE = 88
+
+
+def tile_list_claim_page_scores_kernel(
+    tc, tab_words, tab_scales, offs, offs2, offs3, w1, w4_words, w4_scales, base, gain, wgs, page0, cap, wv, slot, out
+):
+    nc = tc.nc
+    with ExitStack() as ctx:
+        keep = ctx.enter_context(tc.tile_pool(name="keep", bufs=1))
+        ring2 = ctx.enter_context(tc.tile_pool(name="ring2", bufs=2))
+        ring4 = ctx.enter_context(tc.tile_pool(name="ring4", bufs=4))
+        psum = ctx.enter_context(tc.psum_pool(name="psum", bufs=1))
+
+        lists = [keep.tile([P, S // 16], U16, name=f"list{n}") for n in range(3)]
+        tab_sc = keep.tile([P, NA * T], U8, name="tab_sc", align_bytes=64)
+        w4_sc = keep.tile([P, NA * H], U8, name="w4_sc", align_bytes=64)
+        nc.vector.memset(tab_sc[:].bitcast(I32), 0)
+        nc.vector.memset(w4_sc[:].bitcast(I32), 0)
+
+        def load_scales(queue, plane, src):
+            for q in range(4):
+                queue.dma_start(
+                    out=plane[32 * q : 32 * q + 4, :].bitcast(I32).rearrange("r (a c) -> r a c", a=NA),
+                    in_=src[:, 4 * q : 4 * q + 4, :].rearrange("a r c -> r a c").bitcast(I32),
+                )
+
+        base_rows = base.rearrange("(b p t) j -> b t p j", b=NB, t=PACK)
+        page_rows = page0.rearrange("(b p t) m -> b t p m", b=NB, t=PACK)
+        wgs_rows = wgs.rearrange("(p t) j -> p t j", t=PACK)
+
+        tab_w, w1_raw, w4_raw, base_t, page_t = {}, {}, {}, {}, {}
+
+        def load_tab(a):
+            tab_w[a] = keep.tile([P, T], I32, name=f"tab_w{a}", tag=f"big{a}", align_bytes=64)
+            nc.sync.dma_start(out=tab_w[a][:], in_=tab_words[a].rearrange("p t i -> p (t i)").bitcast(I32))
+
+        def load_w1(a, b):
+            w1_raw[a, b] = keep.tile([P, PACK, KP], F32, name=f"w1_raw{a}{b}", tag=f"w1_raw{a}")
+            nc.sync.dma_start(
+                out=w1_raw[a, b][:],
+                in_=w1[KP * a : KP * (a + 1), KP * b : KP * (b + 1)].rearrange("(p i) c -> p i c", i=PACK),
+            )
+
+        def load_w4(b):
+            w4_raw[b] = keep.tile([P, NA * 2 * KP], U8, name=f"w4_raw{b}", tag="w4_raw")
+            nc.sync.dma_start(
+                out=w4_raw[b][:].bitcast(I32).rearrange("p (a c) -> p a c", a=NA),
+                in_=w4_words[:, :, 2 * KP * b : 2 * KP * (b + 1)].rearrange("a p c -> p a c").bitcast(I32),
+            )
+
+        def load_base(s):
+            base_t[s] = ring4.tile([P, S], F32, name=f"base{s}", tag="base")
+            nc.sync.dma_start(out=base_t[s][:], in_=base_rows[s // PACK, s % PACK])
+
+        def load_page(s):
+            page_t[s] = keep.tile([P, T2], F32, name=f"page{s}")
+            nc.sync.dma_start(out=page_t[s][:], in_=page_rows[s // PACK, s % PACK])
+
+        wgs_first = keep.tile([P, S], F32, name="wgs_first")
+        wgs_rest = keep.tile([P, PACK - 1, S], F32, name="wgs_rest")
+        per_row = {n: keep.tile([P, NB, PACK], F32, name=n) for n in ("gain_t", "cap_t", "wv_t")}
+        slot_t = keep.tile([P, NM], F32, name="slot_t")
+
+        def load_rowvec(name, vec):
+            nc.sync.dma_start(out=per_row[name][:], in_=vec.rearrange("(b p t) -> p b t", b=NB, t=PACK))
+
+        nc.sync.dma_start(lists[0][:], offs)
+        nc.sync.dma_start(lists[1][:], offs2)
+        nc.sync.dma_start(lists[2][:], offs3)
+        load_rowvec("gain_t", gain)
+        load_tab(0)
+        load_w1(0, 0)
+        load_rowvec("cap_t", cap)
+        load_rowvec("wv_t", wv)
+        load_scales(nc.sync, tab_sc, tab_scales)
+        load_tab(1)
+        load_scales(nc.sync, w4_sc, w4_scales)
+        load_w4(0)
+        load_w1(1, 0)
+        load_tab(2)
+        load_w1(2, 0)
+        load_base(0)
+        for q in range(4):
+            nc.sync.dma_start(out=wgs_first[32 * q : 32 * (q + 1), :], in_=wgs_rows[:, 0, :])
+        load_page(0)
+        load_base(1)
+        for q in range(4):
+            nc.sync.dma_start(out=wgs_rest[32 * q : 32 * (q + 1), :, :], in_=wgs_rows[:, 1:PACK, :])
+        load_page(1)
+        load_base(2)
+
+        v_codes = [keep.tile([P, S], U32, name=f"v_codes{a}", align_bytes=64) for a in range(NA)]
+        v_scales = [keep.tile([P, S], U8, name=f"v_scales{a}", align_bytes=64) for a in range(NA)]
+        for a in range(NA):
+            nc.vector.tensor_copy(v_scales[a][:], tab_sc[:, T * a : T * (a + 1)].indirect(lists[0][:]))
+
+
+        def gather_tab(a):
+            nc.vector.tensor_copy(v_codes[a][:], tab_w[a][:].bitcast(U32).indirect(lists[0][:]))
+
+        w1_codes, w1_scales, w4_codes, w4_planes = {}, {}, {}, {}
+
+        def quantise_w1(a, b, shared):
+            grouped = ring2.tile([P, PACK * KP], BF16, name=f"w1_grouped{a}{b}", tag="w1_grouped", align_bytes=64)
+            dst = grouped[:].rearrange("p (t c i) -> p c i t", t=PACK, i=PACK)
+            src = w1_raw[a, b][:].rearrange("p i (c t) -> p c i t", t=PACK)
+            if shared:
+                nc.vector.tensor_copy(out=dst[:, :W1_VECTOR_SHARE], in_=src[:, :W1_VECTOR_SHARE])
+                nc.scalar.copy(out=dst[:, W1_VECTOR_SHARE:], in_=src[:, W1_VECTOR_SHARE:])
+            else:
+                nc.scalar.copy(out=dst, in_=src)
+            w1_codes[a, b] = keep.tile([P, KP], U32, name=f"w1_codes{a}{b}", align_bytes=64)
+            w1_scales[a, b] = keep.tile([P, KP], U8, name=f"w1_scales{a}{b}", align_bytes=64)
+            cuts = (0, P, 2 * P, KP) if shared else (0, KP)
+            for lo, hi in zip(cuts, cuts[1:]):
+                nc.vector.quantize_mx(
+                    out=w1_codes[a, b][:, lo:hi].bitcast(FP8X4),
+                    scales=w1_scales[a, b][:, lo:hi],
+                    in_=grouped[:, PACK * lo : PACK * hi],
+                )
+
+        def deal_w4_scales(b):
+            w4_planes[b] = keep.tile([P, NA * KP], U8, name=f"w4_planes{b}", align_bytes=64)
+            nc.vector.tensor_copy(
+                out=w4_planes[b][:].rearrange("p (a t c) -> p t a c", a=NA, t=PACK),
+                in_=w4_sc[:].rearrange("p (a b c t) -> p b t a c", a=NA, b=NB, t=PACK)[:, b],
+            )
+
+        def deal_w4(b):
+            w4_codes[b] = keep.tile([P, NA * 2 * KP], U8, name=f"w4_codes{b}", align_bytes=64)
+            nc.vector.tensor_copy(
+                out=w4_codes[b][:].bitcast(U16).rearrange("p (a t c) -> p t a c", a=NA, t=PACK),
+                in_=w4_raw[b][:].bitcast(U16).rearrange("p (a c t) -> p t a c", a=NA, t=PACK),
+            )
+
+        first, second = {}, {}
+
+        def open_banks(s):
+            first[s] = psum.tile([P, S], F32, name=f"first{s}", tag=f"bank{2 * (s % PACK)}")
+            second[s] = psum.tile([P, S], F32, name=f"second{s}", tag=f"bank{2 * (s % PACK) + 1}")
+
+        def pass_first(s, a):
+            b, t = divmod(s, PACK)
+            nc.tensor.matmul_mx(
+                out=first[s][:],
+                lhsT=w1_codes[a, b][:, P * t : P * (t + 1)].bitcast(FP8X4),
+                lhsT_scale=w1_scales[a, b][:, P * t : P * (t + 1)],
+                rhs=v_codes[a][:].bitcast(FP8X4),
+                rhs_scale=v_scales[a][:],
+                start=(a == 0),
+                stop=(a == NA - 1),
+            )
+
+        def pass_second(s, a):
+            b, t = divmod(s, PACK)
+            c0 = KP * a + P * t
+            nc.tensor.matmul_mx(
+                out=second[s][:],
+                lhsT=w4_codes[b][:, 2 * c0 : 2 * (c0 + P)].bitcast(FP4X4),
+                lhsT_scale=w4_planes[b][:, c0 : c0 + P],
+                rhs=v_codes[a][:].bitcast(FP8X4),
+                rhs_scale=v_scales[a][:],
+                start=(a == 0),
+                stop=(a == NA - 1),
+            )
+
+        tanh_t, max_t, sum_t, wg_t, picked = {}, {}, {}, {}, {}
+
+        def scalar_front(s):
+            b, t = divmod(s, PACK)
+            tanh_t[s] = ring4.tile([P, S], F32, name=f"tanh{s}", tag="tanh")
+            nc.scalar.activation(out=tanh_t[s][:], in_=first[s][:], func=ACT.Tanh)
+            wg_t[s] = ring2.tile([P, S], F32, name=f"wg{s}", tag="wg")
+            rows = wgs_first[:] if t == 0 else wgs_rest[:, t - 1, :]
+            nc.scalar.activation(out=wg_t[s][:], in_=rows, func=ACT.Copy, scale=per_row["gain_t"][:, b, t : t + 1])
+
+        def take_max(s):
+            max_t[s] = ring2.tile([P, S], F32, name=f"max{s}", tag="max")
+            nc.vector.tensor_tensor(max_t[s][:], second[s][:], base_t[s][:], ALU.max)
+
+        def take_sum(s):
+            sum_t[s] = ring2.tile([P, S], F32, name=f"sum{s}", tag="sum")
+            nc.vector.tensor_tensor(sum_t[s][:], tanh_t[s][:], max_t[s][:], ALU.add)
+
+        def scatter(s):
+            nc.vector.tensor_tensor(page_t[s][:].indirect(lists[1][:]), sum_t[s][:], wg_t[s][:], ALU.mult)
+
+        def pick(s):
+            picked[s] = ring2.tile([P, PJ], F32, name=f"picked{s}", tag="picked")
+            nc.vector.tensor_copy(picked[s][:], page_t[s][:].indirect(lists[2][:]))
+
+        planes_in = (PACK, 2)
+        page_planes = [keep.tile([P, planes_in[b], T2], BF16, name=f"page_planes{b}") for b in range(NB)]
+        x_planes = [keep.tile([P, planes_in[b], PJ], BF16, name=f"x_planes{b}") for b in range(NB)]
+        page_grouped = [keep.tile([P, T2 * PACK], BF16, name=f"page_grouped{b}", align_bytes=64) for b in range(NB)]
+        x_grouped = [keep.tile([P, PJ * PACK], BF16, name=f"x_grouped{b}", align_bytes=64) for b in range(NB)]
+        page_codes = [keep.tile([P, T2], U32, name=f"page_codes{b}", align_bytes=64) for b in range(NB)]
+        page_scales = [keep.tile([P, T2], U8, name=f"page_scales{b}", align_bytes=64) for b in range(NB)]
+        x_codes = [keep.tile([P, PJ], U32, name=f"x_codes{b}", align_bytes=64) for b in range(NB)]
+        x_scales = [keep.tile([P, PJ], U8, name=f"x_scales{b}", align_bytes=64) for b in range(NB)]
+        PIECE = 256
+
+        def cap_and_weigh(s):
+            b, t = divmod(s, PACK)
+            if t < planes_in[b]:
+                dst = x_planes[b][:, t, :]
+            else:
+                dst = x_grouped[b][:].rearrange("p (j t) -> p t j", t=PACK)[:, t, :]
+            nc.vector.tensor_scalar(
+                dst, picked[s][:], per_row["cap_t"][:, b, t : t + 1], per_row["wv_t"][:, b, t : t + 1], ALU.min, ALU.mult
+            )
+
+        def round_page(s):
+            b, t = divmod(s, PACK)
+            if t < planes_in[b]:
+                nc.scalar.copy(out=page_planes[b][:, t, :], in_=page_t[s][:])
+            else:
+                dst = page_grouped[b][:].rearrange("p (m t) -> p t m", t=PACK)[:, t, :]
+                for m0 in range(0, T2, PIECE):
+                    nc.scalar.copy(out=dst[:, m0 : m0 + PIECE], in_=page_t[s][:, m0 : m0 + PIECE])
+
+        def weave(planes, grouped, n_planes, width):
+            dst = grouped[:].rearrange("p (c i t) -> p c t i", i=4, t=PACK)[:, :, :n_planes, :]
+            src = planes[:].rearrange("p t (c i) -> p c t i", i=4)
+            for c0 in range(0, width // 4, PIECE // 4):
+                nc.scalar.copy(out=dst[:, c0 : c0 + PIECE // 4], in_=src[:, c0 : c0 + PIECE // 4])
+
+        def quantise_x(b):
+            nc.vector.quantize_mx(out=x_codes[b][:].bitcast(FP8X4), scales=x_scales[b][:], in_=x_grouped[b][:])
+
+        def quantise_page(b, m0, width):
+            nc.vector.quantize_mx(
+                out=page_codes[b][:, m0 : m0 + width].bitcast(FP8X4),
+                scales=page_scales[b][:, m0 : m0 + width],
+                in_=page_grouped[b][:, PACK * m0 : PACK * (m0 + width)],
+            )
+
+        for s in range(PACK):
+            open_banks(s)
+        for a in range(NA):
+            gather_tab(a)
+            if a == 0:
+                deal_w4_scales(0)
+                deal_w4(0)
+                deal_w4_scales(1)
+            quantise_w1(a, 0, shared=(a == NA - 1))
+        for s in range(PACK):
+            for a in range(NA):
+                pass_second(s, a)
+                pass_first(s, a)
+
+        load_w1(0, 1)
+        load_page(2)
+        load_base(3)
+        load_w1(1, 1)
+        load_w1(2, 1)
+        load_w4(1)
+
+        scalar_front(0)
+        take_max(0)
+        take_sum(0)
+        for s in range(NS):
+            b, t = divmod(s, PACK)
+            nxt = s + 1
+            if s < NA:
+                quantise_w1(s, 1, shared=False)
+            if s == NA - 1:
+                deal_w4(1)
+                load_base(4)
+                load_page(3)
+            if nxt == PACK:
+                for s2 in range(PACK, NS):
+                    if s2 > PACK:
+                        load_base(s2)
+                    load_page(s2)
+                with nc.allow_non_contiguous_dma(reason="one floor a partition"):
+                    nc.sync.dma_start(out=slot_t[:], in_=slot.rearrange("(i p) -> p i", p=P))
+            if PACK <= nxt < NS:
+                open_banks(nxt)
+                for a in range(NA):
+                    pass_second(nxt, a)
+                    pass_first(nxt, a)
+            if nxt < NS:
+                scalar_front(nxt)
+            scatter(s)
+            if nxt < NS:
+                take_max(nxt)
+            pick(s)
+            if nxt < NS:
+                take_sum(nxt)
+            cap_and_weigh(s)
+            round_page(s)
+            if t == planes_in[b] - 1:
+                weave(x_planes[b], x_grouped[b], planes_in[b], PJ)
+                weave(page_planes[b], page_grouped[b], planes_in[b], T2)
+            if s == PACK + 1:
+                quantise_x(0)
+                quantise_page(0, 0, T2)
+
+        scores = [psum.tile([P, PJ], F32, name=f"scores{m}", tag=f"bank{m}") for m in range(NM)]
+
+        def pass_scores(m, b):
+            nc.tensor.matmul_mx(
+                out=scores[m][:],
+                lhsT=page_codes[b][:, P * m : P * (m + 1)].bitcast(FP8X4),
+                lhsT_scale=page_scales[b][:, P * m : P * (m + 1)],
+                rhs=x_codes[b][:].bitcast(FP8X4),
+                rhs_scale=x_scales[b][:],
+                start=(b == 0),
+                stop=(b == NB - 1),
+            )
+
+        for m in range(NM):
+            pass_scores(m, 0)
+        quantise_x(1)
+        staged = [keep.tile([P, PACK, PJ], F32, name=f"staged{n}", tag=f"big{n}", align_bytes=64) for n in range(2)]
+        for m in range(NM):
+            if (P * m) % PIECE == 0:
+                quantise_page(1, P * m, PIECE)
+            pass_scores(m, 1)
+            row = staged[m // PACK][:, m % PACK, :]
+            nc.vector.tensor_scalar(row, scores[m][:], slot_t[:, m : m + 1], None, ALU.max)
+            nc.scalar.activation(out=row, in_=row, func=ACT.Ln)
+            nc.sync.dma_start(out=out[P * m : P * (m + 1), :], in_=row)

@@ -39,7 +39,9 @@ def tile_list_claim_page_scores_kernel(
         lists = [keep.tile([P, S // 16], U16, name=f"list{n}") for n in range(3)]
         tab_sc = keep.tile([P, NA * T], U8, name="tab_sc", align_bytes=64)
         w4_sc = keep.tile([P, NA * H], U8, name="w4_sc", align_bytes=64)
-        nc.vector.memset(tab_sc[:].bitcast(I32), 0)
+        half = NA * T // 2
+        nc.vector.memset(tab_sc[:, :half].bitcast(I32), 0)
+        nc.gpsimd.memset(tab_sc[:, half:].bitcast(I32), 0)
         nc.vector.memset(w4_sc[:].bitcast(I32), 0)
 
         def load_scales(queue, plane, src):
@@ -93,11 +95,13 @@ def tile_list_claim_page_scores_kernel(
         nc.sync.dma_start(lists[1][:], offs2)
         nc.sync.dma_start(lists[2][:], offs3)
         load_rowvec("gain_t", gain)
-        load_tab(0)
-        load_w1(0, 0)
         load_rowvec("cap_t", cap)
         load_rowvec("wv_t", wv)
+        with nc.allow_non_contiguous_dma(reason="one floor a partition"):
+            nc.sync.dma_start(out=slot_t[:], in_=slot.rearrange("(i p) -> p i", p=P))
+        load_tab(0)
         load_scales(nc.sync, tab_sc, tab_scales)
+        load_w1(0, 0)
         load_tab(1)
         load_scales(nc.sync, w4_sc, w4_scales)
         load_w4(0)
@@ -107,12 +111,13 @@ def tile_list_claim_page_scores_kernel(
         load_base(0)
         for q in range(4):
             nc.sync.dma_start(out=wgs_first[32 * q : 32 * (q + 1), :], in_=wgs_rows[:, 0, :])
-        load_page(0)
         load_base(1)
+        load_page(0)
+        load_base(2)
         for q in range(4):
             nc.sync.dma_start(out=wgs_rest[32 * q : 32 * (q + 1), :, :], in_=wgs_rows[:, 1:PACK, :])
+        load_base(3)
         load_page(1)
-        load_base(2)
 
         v_codes = [keep.tile([P, S], U32, name=f"v_codes{a}", align_bytes=64) for a in range(NA)]
         v_scales = [keep.tile([P, S], U8, name=f"v_scales{a}", align_bytes=64) for a in range(NA)]
@@ -161,8 +166,8 @@ def tile_list_claim_page_scores_kernel(
         first, second = {}, {}
 
         def open_banks(s):
-            first[s] = psum.tile([P, S], F32, name=f"first{s}", tag=f"bank{2 * (s % PACK)}")
-            second[s] = psum.tile([P, S], F32, name=f"second{s}", tag=f"bank{2 * (s % PACK) + 1}")
+            first[s] = psum.tile([P, S], F32, name=f"first{s}", tag=f"bank{2 * (s % 2)}")
+            second[s] = psum.tile([P, S], F32, name=f"second{s}", tag=f"bank{2 * (s % 2) + 1}")
 
         def pass_first(s, a):
             b, t = divmod(s, PACK)
@@ -189,23 +194,27 @@ def tile_list_claim_page_scores_kernel(
                 stop=(a == NA - 1),
             )
 
-        tanh_t, max_t, sum_t, wg_t, picked = {}, {}, {}, {}, {}
+        tanh_t, sum_t, wg_t, picked = {}, {}, {}, {}
 
-        def scalar_front(s):
-            b, t = divmod(s, PACK)
-            tanh_t[s] = ring4.tile([P, S], F32, name=f"tanh{s}", tag="tanh")
+        def first_stage(s):
+            open_banks(s)
+            for a in range(NA):
+                pass_second(s, a)
+                pass_first(s, a)
+            tanh_t[s] = ring2.tile([P, S], F32, name=f"tanh{s}", tag="tanh")
             nc.scalar.activation(out=tanh_t[s][:], in_=first[s][:], func=ACT.Tanh)
+
+        def weigh_gain(s):
+            b, t = divmod(s, PACK)
             wg_t[s] = ring2.tile([P, S], F32, name=f"wg{s}", tag="wg")
             rows = wgs_first[:] if t == 0 else wgs_rest[:, t - 1, :]
             nc.scalar.activation(out=wg_t[s][:], in_=rows, func=ACT.Copy, scale=per_row["gain_t"][:, b, t : t + 1])
 
-        def take_max(s):
-            max_t[s] = ring2.tile([P, S], F32, name=f"max{s}", tag="max")
-            nc.vector.tensor_tensor(max_t[s][:], second[s][:], base_t[s][:], ALU.max)
-
-        def take_sum(s):
+        def max_and_sum(s):
             sum_t[s] = ring2.tile([P, S], F32, name=f"sum{s}", tag="sum")
-            nc.vector.tensor_tensor(sum_t[s][:], tanh_t[s][:], max_t[s][:], ALU.add)
+            nc.vector.tensor_tensor(sum_t[s][:], second[s][:], base_t[s][:], ALU.max)
+            adder = nc.vector if s == 0 else nc.gpsimd
+            adder.tensor_tensor(sum_t[s][:], sum_t[s][:], tanh_t[s][:], ALU.add)
 
         def scatter(s):
             nc.vector.tensor_tensor(page_t[s][:].indirect(lists[1][:]), sum_t[s][:], wg_t[s][:], ALU.mult)
@@ -260,59 +269,41 @@ def tile_list_claim_page_scores_kernel(
                 in_=page_grouped[b][:, PACK * m0 : PACK * (m0 + width)],
             )
 
-        for s in range(PACK):
-            open_banks(s)
         for a in range(NA):
             gather_tab(a)
+            quantise_w1(a, 0, shared=(a == NA - 1))
             if a == 0:
                 deal_w4_scales(0)
                 deal_w4(0)
-                deal_w4_scales(1)
-            quantise_w1(a, 0, shared=(a == NA - 1))
-        for s in range(PACK):
-            for a in range(NA):
-                pass_second(s, a)
-                pass_first(s, a)
-
-        load_w1(0, 1)
-        load_page(2)
-        load_base(3)
-        load_w1(1, 1)
-        load_w1(2, 1)
+        for a in range(NA):
+            load_w1(a, 1)
         load_w4(1)
 
-        scalar_front(0)
-        take_max(0)
-        take_sum(0)
+        for s in range(2):
+            first_stage(s)
+            weigh_gain(s)
+            max_and_sum(s)
         for s in range(NS):
             b, t = divmod(s, PACK)
-            nxt = s + 1
-            if s < NA:
-                quantise_w1(s, 1, shared=False)
-            if s == NA - 1:
-                deal_w4(1)
-                load_base(4)
-                load_page(3)
-            if nxt == PACK:
-                for s2 in range(PACK, NS):
-                    if s2 > PACK:
-                        load_base(s2)
-                    load_page(s2)
-                with nc.allow_non_contiguous_dma(reason="one floor a partition"):
-                    nc.sync.dma_start(out=slot_t[:], in_=slot.rearrange("(i p) -> p i", p=P))
-            if PACK <= nxt < NS:
-                open_banks(nxt)
+            ahead = s + 2
+            if s == 1:
                 for a in range(NA):
-                    pass_second(nxt, a)
-                    pass_first(nxt, a)
-            if nxt < NS:
-                scalar_front(nxt)
+                    quantise_w1(a, 1, shared=False)
+                deal_w4_scales(1)
+                deal_w4(1)
+            if PACK <= ahead < NS:
+                load_base(ahead)
+            if ahead < NS:
+                load_page(ahead)
+                first_stage(ahead)
+            if ahead == NS - 1:
+                warm = keep.tile([P, 1], F32, name="warm")
+                nc.scalar.activation(out=warm[:], in_=tanh_t[ahead][:, 0:1], func=ACT.Ln, scale=0.0, bias=1.0)
             scatter(s)
-            if nxt < NS:
-                take_max(nxt)
+            if ahead < NS:
+                weigh_gain(ahead)
+                max_and_sum(ahead)
             pick(s)
-            if nxt < NS:
-                take_sum(nxt)
             cap_and_weigh(s)
             round_page(s)
             if t == planes_in[b] - 1:
@@ -322,7 +313,7 @@ def tile_list_claim_page_scores_kernel(
                 quantise_x(0)
                 quantise_page(0, 0, T2)
 
-        scores = [psum.tile([P, PJ], F32, name=f"scores{m}", tag=f"bank{m}") for m in range(NM)]
+        scores = [psum.tile([P, PJ], F32, name=f"scores{m}", tag=f"bank{(m + PACK) % NM}") for m in range(NM)]
 
         def pass_scores(m, b):
             nc.tensor.matmul_mx(

@@ -97,26 +97,23 @@ def tile_list_claim_page_scores_kernel(
         load_rowvec("gain_t", gain)
         load_rowvec("cap_t", cap)
         load_rowvec("wv_t", wv)
-        with nc.allow_non_contiguous_dma(reason="one floor a partition"):
-            nc.sync.dma_start(out=slot_t[:], in_=slot.rearrange("(i p) -> p i", p=P))
         load_tab(0)
         load_scales(nc.sync, tab_sc, tab_scales)
         load_w1(0, 0)
-        load_tab(1)
         load_scales(nc.sync, w4_sc, w4_scales)
         load_w4(0)
+        load_tab(1)
         load_w1(1, 0)
         load_tab(2)
         load_w1(2, 0)
         load_base(0)
-        for q in range(4):
+        for q in (0, 2, 1, 3):
             nc.sync.dma_start(out=wgs_first[32 * q : 32 * (q + 1), :], in_=wgs_rows[:, 0, :])
-        load_base(1)
         load_page(0)
-        load_base(2)
-        for q in range(4):
+        load_base(1)
+        for q in (0, 2, 1, 3):
             nc.sync.dma_start(out=wgs_rest[32 * q : 32 * (q + 1), :, :], in_=wgs_rows[:, 1:PACK, :])
-        load_base(3)
+        load_base(2)
         load_page(1)
 
         v_codes = [keep.tile([P, S], U32, name=f"v_codes{a}", align_bytes=64) for a in range(NA)]
@@ -194,14 +191,14 @@ def tile_list_claim_page_scores_kernel(
                 stop=(a == NA - 1),
             )
 
-        tanh_t, sum_t, wg_t, picked = {}, {}, {}, {}
+        tanh_t, larger, sum_t, wg_t, picked = {}, {}, {}, {}, {}
 
         def first_stage(s):
             open_banks(s)
             for a in range(NA):
                 pass_second(s, a)
                 pass_first(s, a)
-            tanh_t[s] = ring2.tile([P, S], F32, name=f"tanh{s}", tag="tanh")
+            tanh_t[s] = ring4.tile([P, S], F32, name=f"tanh{s}", tag="tanh")
             nc.scalar.activation(out=tanh_t[s][:], in_=first[s][:], func=ACT.Tanh)
 
         def weigh_gain(s):
@@ -210,11 +207,13 @@ def tile_list_claim_page_scores_kernel(
             rows = wgs_first[:] if t == 0 else wgs_rest[:, t - 1, :]
             nc.scalar.activation(out=wg_t[s][:], in_=rows, func=ACT.Copy, scale=per_row["gain_t"][:, b, t : t + 1])
 
-        def max_and_sum(s):
+        def take_max(s):
+            larger[s] = ring2.tile([P, S], F32, name=f"larger{s}", tag="larger")
+            nc.vector.tensor_tensor(larger[s][:], second[s][:], base_t[s][:], ALU.max)
+
+        def take_sum(s):
             sum_t[s] = ring2.tile([P, S], F32, name=f"sum{s}", tag="sum")
-            nc.vector.tensor_tensor(sum_t[s][:], second[s][:], base_t[s][:], ALU.max)
-            adder = nc.vector if s == 0 else nc.gpsimd
-            adder.tensor_tensor(sum_t[s][:], sum_t[s][:], tanh_t[s][:], ALU.add)
+            nc.vector.tensor_tensor(sum_t[s][:], larger[s][:], tanh_t[s][:], ALU.add)
 
         def scatter(s):
             nc.vector.tensor_tensor(page_t[s][:].indirect(lists[1][:]), sum_t[s][:], wg_t[s][:], ALU.mult)
@@ -275,35 +274,48 @@ def tile_list_claim_page_scores_kernel(
             if a == 0:
                 deal_w4_scales(0)
                 deal_w4(0)
-        for a in range(NA):
-            load_w1(a, 1)
+        load_w1(0, 1)
+        load_base(3)
+        load_page(2)
+        load_w1(1, 1)
+        load_w1(2, 1)
         load_w4(1)
 
-        for s in range(2):
-            first_stage(s)
-            weigh_gain(s)
-            max_and_sum(s)
+        first_stage(0)
+        weigh_gain(0)
+        take_max(0)
+        take_sum(0)
+        first_stage(1)
+        weigh_gain(1)
         for s in range(NS):
             b, t = divmod(s, PACK)
-            ahead = s + 2
+            nxt, ahead = s + 1, s + 2
             if s == 1:
                 for a in range(NA):
                     quantise_w1(a, 1, shared=False)
                 deal_w4_scales(1)
                 deal_w4(1)
+                load_base(PACK)
+                load_page(3)
             if PACK <= ahead < NS:
-                load_base(ahead)
-            if ahead < NS:
+                if ahead > PACK:
+                    load_base(ahead)
                 load_page(ahead)
+            if ahead < NS:
                 first_stage(ahead)
             if ahead == NS - 1:
+                with nc.allow_non_contiguous_dma(reason="one floor a partition"):
+                    nc.sync.dma_start(out=slot_t[:], in_=slot.rearrange("(i p) -> p i", p=P))
                 warm = keep.tile([P, 1], F32, name="warm")
                 nc.scalar.activation(out=warm[:], in_=tanh_t[ahead][:, 0:1], func=ACT.Ln, scale=0.0, bias=1.0)
             scatter(s)
             if ahead < NS:
                 weigh_gain(ahead)
-                max_and_sum(ahead)
+            if nxt < NS:
+                take_max(nxt)
             pick(s)
+            if nxt < NS:
+                take_sum(nxt)
             cap_and_weigh(s)
             round_page(s)
             if t == planes_in[b] - 1:

from contextlib import ExitStack

import concourse.mybir as mybir

K, H, T, S, T2, PJ = 1536, 1024, 2048, 512, 1024, 512
FLOPS = 2 * (2 * K * H * S + H * T2 * PJ)

F32 = mybir.dt.float32
BF16 = mybir.dt.bfloat16
I32 = mybir.dt.int32
U32 = mybir.dt.uint32
U16 = mybir.dt.uint16
U8 = mybir.dt.uint8
FP8X4 = mybir.dt.float8_e4m3fn_x4
FP4X4 = mybir.dt.float4_e2m1fn_x4
ALU = mybir.AluOpType
ACT = mybir.ActivationFunctionType

P = 128
PACK = 4
KP = P * PACK
NA = K // KP
NB = H // KP
NS = NB * PACK
NM = T2 // P
W1_VECTOR_SHARE = 88


def tile_list_claim_page_scores_kernel(
    tc, tab_words, tab_scales, offs, offs2, offs3, w1, w4_words, w4_scales, base, gain, wgs, page0, cap, wv, slot, out
):
    nc = tc.nc
    with ExitStack() as ctx:
        keep = ctx.enter_context(tc.tile_pool(name="keep", bufs=1))
        ring2 = ctx.enter_context(tc.tile_pool(name="ring2", bufs=2))
        ring4 = ctx.enter_context(tc.tile_pool(name="ring4", bufs=4))
        psum = ctx.enter_context(tc.psum_pool(name="psum", bufs=1))

        lists = [keep.tile([P, S // 16], U16, name=f"list{n}") for n in range(3)]
        tab_sc = keep.tile([P, NA * T], U8, name="tab_sc", align_bytes=64)
        w4_sc = keep.tile([P, NA * H], U8, name="w4_sc", align_bytes=64)
        half = NA * T // 2
        nc.vector.memset(tab_sc[:, :half].bitcast(I32), 0)
        nc.gpsimd.memset(tab_sc[:, half:].bitcast(I32), 0)
        nc.vector.memset(w4_sc[:].bitcast(I32), 0)

        def load_scales(queue, plane, src):
            for q in range(4):
                queue.dma_start(
                    out=plane[32 * q : 32 * q + 4, :].bitcast(I32).rearrange("r (a c) -> r a c", a=NA),
                    in_=src[:, 4 * q : 4 * q + 4, :].rearrange("a r c -> r a c").bitcast(I32),
                )

        base_rows = base.rearrange("(b p t) j -> b t p j", b=NB, t=PACK)
        page_rows = page0.rearrange("(b p t) m -> b t p m", b=NB, t=PACK)
        wgs_rows = wgs.rearrange("(p t) j -> p t j", t=PACK)

        tab_w, w1_raw, w4_raw, base_t, page_t = {}, {}, {}, {}, {}

        def load_tab(a):
            tab_w[a] = keep.tile([P, T], I32, name=f"tab_w{a}", tag=f"big{a}", align_bytes=64)
            nc.sync.dma_start(out=tab_w[a][:], in_=tab_words[a].rearrange("p t i -> p (t i)").bitcast(I32))

        def load_w1(a, b):
            w1_raw[a, b] = keep.tile([P, PACK, KP], F32, name=f"w1_raw{a}{b}", tag=f"w1_raw{a}")
            nc.sync.dma_start(
                out=w1_raw[a, b][:],
                in_=w1[KP * a : KP * (a + 1), KP * b : KP * (b + 1)].rearrange("(p i) c -> p i c", i=PACK),
            )

        def load_w4(b):
            w4_raw[b] = keep.tile([P, NA * 2 * KP], U8, name=f"w4_raw{b}", tag="w4_raw")
            nc.sync.dma_start(
                out=w4_raw[b][:].bitcast(I32).rearrange("p (a c) -> p a c", a=NA),
                in_=w4_words[:, :, 2 * KP * b : 2 * KP * (b + 1)].rearrange("a p c -> p a c").bitcast(I32),
            )

        def load_base(s):
            base_t[s] = ring4.tile([P, S], F32, name=f"base{s}", tag="base")
            nc.sync.dma_start(out=base_t[s][:], in_=base_rows[s // PACK, s % PACK])

        def load_page(s):
            page_t[s] = keep.tile([P, T2], F32, name=f"page{s}")
            nc.sync.dma_start(out=page_t[s][:], in_=page_rows[s // PACK, s % PACK])

        wgs_first = keep.tile([P, S], F32, name="wgs_first")
        wgs_rest = keep.tile([P, PACK - 1, S], F32, name="wgs_rest")
        per_row = {n: keep.tile([P, NB, PACK], F32, name=n) for n in ("gain_t", "cap_t", "wv_t")}
        slot_t = keep.tile([P, NM], F32, name="slot_t")

        def load_rowvec(name, vec):
            nc.sync.dma_start(out=per_row[name][:], in_=vec.rearrange("(b p t) -> p b t", b=NB, t=PACK))

        nc.sync.dma_start(lists[0][:], offs)
        nc.sync.dma_start(lists[1][:], offs2)
        nc.sync.dma_start(lists[2][:], offs3)
        load_rowvec("gain_t", gain)
        load_rowvec("cap_t", cap)
        load_rowvec("wv_t", wv)
        load_tab(0)
        load_scales(nc.sync, tab_sc, tab_scales)
        load_w1(0, 0)
        load_scales(nc.sync, w4_sc, w4_scales)
        load_w4(0)
        load_tab(1)
        load_w1(1, 0)
        load_tab(2)
        load_w1(2, 0)
        load_base(0)
        for q in (0, 2, 1, 3):
            nc.sync.dma_start(out=wgs_first[32 * q : 32 * (q + 1), :], in_=wgs_rows[:, 0, :])
        load_page(0)
        load_base(1)
        for q in (0, 2, 1, 3):
            nc.sync.dma_start(out=wgs_rest[32 * q : 32 * (q + 1), :, :], in_=wgs_rows[:, 1:PACK, :])
        load_base(2)
        load_page(1)

        v_codes = [keep.tile([P, S], U32, name=f"v_codes{a}", align_bytes=64) for a in range(NA)]
        v_scales = [keep.tile([P, S], U8, name=f"v_scales{a}", align_bytes=64) for a in range(NA)]
        for a in range(NA):
            nc.vector.tensor_copy(v_scales[a][:], tab_sc[:, T * a : T * (a + 1)].indirect(lists[0][:]))


        def gather_tab(a):
            nc.vector.tensor_copy(v_codes[a][:], tab_w[a][:].bitcast(U32).indirect(lists[0][:]))

        w1_codes, w1_scales, w4_codes, w4_planes = {}, {}, {}, {}

        def quantise_w1(a, b, shared):
            grouped = ring2.tile([P, PACK * KP], BF16, name=f"w1_grouped{a}{b}", tag="w1_grouped", align_bytes=64)
            dst = grouped[:].rearrange("p (t c i) -> p c i t", t=PACK, i=PACK)
            src = w1_raw[a, b][:].rearrange("p i (c t) -> p c i t", t=PACK)
            if shared:
                nc.vector.tensor_copy(out=dst[:, :W1_VECTOR_SHARE], in_=src[:, :W1_VECTOR_SHARE])
                nc.scalar.copy(out=dst[:, W1_VECTOR_SHARE:], in_=src[:, W1_VECTOR_SHARE:])
            else:
                nc.scalar.copy(out=dst, in_=src)
            w1_codes[a, b] = keep.tile([P, KP], U32, name=f"w1_codes{a}{b}", align_bytes=64)
            w1_scales[a, b] = keep.tile([P, KP], U8, name=f"w1_scales{a}{b}", align_bytes=64)
            cuts = (0, P, 2 * P, KP) if shared else (0, KP)
            for lo, hi in zip(cuts, cuts[1:]):
                nc.vector.quantize_mx(
                    out=w1_codes[a, b][:, lo:hi].bitcast(FP8X4),
                    scales=w1_scales[a, b][:, lo:hi],
                    in_=grouped[:, PACK * lo : PACK * hi],
                )

        def deal_w4_scales(b):
            w4_planes[b] = keep.tile([P, NA * KP], U8, name=f"w4_planes{b}", align_bytes=64)
            nc.vector.tensor_copy(
                out=w4_planes[b][:].rearrange("p (a t c) -> p t a c", a=NA, t=PACK),
                in_=w4_sc[:].rearrange("p (a b c t) -> p b t a c", a=NA, b=NB, t=PACK)[:, b],
            )

        def deal_w4(b):
            w4_codes[b] = keep.tile([P, NA * 2 * KP], U8, name=f"w4_codes{b}", align_bytes=64)
            nc.vector.tensor_copy(
                out=w4_codes[b][:].bitcast(U16).rearrange("p (a t c) -> p t a c", a=NA, t=PACK),
                in_=w4_raw[b][:].bitcast(U16).rearrange("p (a c t) -> p t a c", a=NA, t=PACK),
            )

        first, second = {}, {}

        def open_banks(s):
            first[s] = psum.tile([P, S], F32, name=f"first{s}", tag=f"bank{2 * (s % 2)}")
            second[s] = psum.tile([P, S], F32, name=f"second{s}", tag=f"bank{2 * (s % 2) + 1}")

        def pass_first(s, a):
            b, t = divmod(s, PACK)
            nc.tensor.matmul_mx(
                out=first[s][:],
                lhsT=w1_codes[a, b][:, P * t : P * (t + 1)].bitcast(FP8X4),
                lhsT_scale=w1_scales[a, b][:, P * t : P * (t + 1)],
                rhs=v_codes[a][:].bitcast(FP8X4),
                rhs_scale=v_scales[a][:],
                start=(a == 0),
                stop=(a == NA - 1),
            )

        def pass_second(s, a):
            b, t = divmod(s, PACK)
            c0 = KP * a + P * t
            nc.tensor.matmul_mx(
                out=second[s][:],
                lhsT=w4_codes[b][:, 2 * c0 : 2 * (c0 + P)].bitcast(FP4X4),
                lhsT_scale=w4_planes[b][:, c0 : c0 + P],
                rhs=v_codes[a][:].bitcast(FP8X4),
                rhs_scale=v_scales[a][:],
                start=(a == 0),
                stop=(a == NA - 1),
            )

        tanh_t, larger, sum_t, wg_t, picked = {}, {}, {}, {}, {}

        def first_stage(s):
            open_banks(s)
            for a in range(NA):
                pass_second(s, a)
                pass_first(s, a)
            tanh_t[s] = ring4.tile([P, S], F32, name=f"tanh{s}", tag="tanh")
            nc.scalar.activation(out=tanh_t[s][:], in_=first[s][:], func=ACT.Tanh)

        def weigh_gain(s):
            b, t = divmod(s, PACK)
            wg_t[s] = ring2.tile([P, S], F32, name=f"wg{s}", tag="wg")
            rows = wgs_first[:] if t == 0 else wgs_rest[:, t - 1, :]
            nc.scalar.activation(out=wg_t[s][:], in_=rows, func=ACT.Copy, scale=per_row["gain_t"][:, b, t : t + 1])

        def take_max(s):
            larger[s] = ring2.tile([P, S], F32, name=f"larger{s}", tag="larger")
            nc.vector.tensor_tensor(larger[s][:], second[s][:], base_t[s][:], ALU.max)

        def take_sum(s):
            sum_t[s] = ring2.tile([P, S], F32, name=f"sum{s}", tag="sum")
            nc.vector.tensor_tensor(sum_t[s][:], larger[s][:], tanh_t[s][:], ALU.add)

        def scatter(s):
            nc.vector.tensor_tensor(page_t[s][:].indirect(lists[1][:]), sum_t[s][:], wg_t[s][:], ALU.mult)

        def pick(s):
            picked[s] = ring2.tile([P, PJ], F32, name=f"picked{s}", tag="picked")
            nc.vector.tensor_copy(picked[s][:], page_t[s][:].indirect(lists[2][:]))

        planes_in = (PACK, 2)
        page_planes = [keep.tile([P, planes_in[b], T2], BF16, name=f"page_planes{b}") for b in range(NB)]
        x_planes = [keep.tile([P, planes_in[b], PJ], BF16, name=f"x_planes{b}") for b in range(NB)]
        page_grouped = [keep.tile([P, T2 * PACK], BF16, name=f"page_grouped{b}", align_bytes=64) for b in range(NB)]
        x_grouped = [keep.tile([P, PJ * PACK], BF16, name=f"x_grouped{b}", align_bytes=64) for b in range(NB)]
        page_codes = [keep.tile([P, T2], U32, name=f"page_codes{b}", align_bytes=64) for b in range(NB)]
        page_scales = [keep.tile([P, T2], U8, name=f"page_scales{b}", align_bytes=64) for b in range(NB)]
        x_codes = [keep.tile([P, PJ], U32, name=f"x_codes{b}", align_bytes=64) for b in range(NB)]
        x_scales = [keep.tile([P, PJ], U8, name=f"x_scales{b}", align_bytes=64) for b in range(NB)]
        PIECE = 256

        def cap_and_weigh(s):
            b, t = divmod(s, PACK)
            if t < planes_in[b]:
                dst = x_planes[b][:, t, :]
            else:
                dst = x_grouped[b][:].rearrange("p (j t) -> p t j", t=PACK)[:, t, :]
            nc.vector.tensor_scalar(
                dst, picked[s][:], per_row["cap_t"][:, b, t : t + 1], per_row["wv_t"][:, b, t : t + 1], ALU.min, ALU.mult
            )

        def round_page(s):
            b, t = divmod(s, PACK)
            if t < planes_in[b]:
                nc.scalar.copy(out=page_planes[b][:, t, :], in_=page_t[s][:])
            else:
                dst = page_grouped[b][:].rearrange("p (m t) -> p t m", t=PACK)[:, t, :]
                for m0 in range(0, T2, PIECE):
                    nc.scalar.copy(out=dst[:, m0 : m0 + PIECE], in_=page_t[s][:, m0 : m0 + PIECE])

        def weave(planes, grouped, n_planes, width):
            dst = grouped[:].rearrange("p (c i t) -> p c t i", i=4, t=PACK)[:, :, :n_planes, :]
            src = planes[:].rearrange("p t (c i) -> p c t i", i=4)
            for c0 in range(0, width // 4, PIECE // 4):
                nc.scalar.copy(out=dst[:, c0 : c0 + PIECE // 4], in_=src[:, c0 : c0 + PIECE // 4])

        def quantise_x(b):
            nc.vector.quantize_mx(out=x_codes[b][:].bitcast(FP8X4), scales=x_scales[b][:], in_=x_grouped[b][:])

        def quantise_page(b, m0, width):
            nc.vector.quantize_mx(
                out=page_codes[b][:, m0 : m0 + width].bitcast(FP8X4),
                scales=page_scales[b][:, m0 : m0 + width],
                in_=page_grouped[b][:, PACK * m0 : PACK * (m0 + width)],
            )

        for a in range(NA):
            gather_tab(a)
            quantise_w1(a, 0, shared=(a == NA - 1))
            if a == 0:
                deal_w4_scales(0)
                deal_w4(0)
        load_w1(0, 1)
        load_base(3)
        load_page(2)
        load_w1(1, 1)
        load_w1(2, 1)
        load_w4(1)

        first_stage(0)
        weigh_gain(0)
        take_max(0)
        take_sum(0)
        first_stage(1)
        weigh_gain(1)
        for s in range(NS):
            b, t = divmod(s, PACK)
            nxt, ahead = s + 1, s + 2
            if s == 1:
                for a in range(NA):
                    quantise_w1(a, 1, shared=False)
                deal_w4_scales(1)
                deal_w4(1)
                load_base(PACK)
                load_page(3)
            if PACK <= ahead < NS:
                if ahead > PACK:
                    load_base(ahead)
                load_page(ahead)
            if ahead < NS:
                first_stage(ahead)
            if ahead == NS - 1:
                with nc.allow_non_contiguous_dma(reason="one floor a partition"):
                    nc.sync.dma_start(out=slot_t[:], in_=slot.rearrange("(i p) -> p i", p=P))
                warm = keep.tile([P, 1], F32, name="warm")
                nc.scalar.activation(out=warm[:], in_=tanh_t[ahead][:, 0:1], func=ACT.Ln, scale=0.0, bias=1.0)
            scatter(s)
            if ahead < NS:
                weigh_gain(ahead)
            if nxt < NS:
                take_max(nxt)
            pick(s)
            if nxt < NS:
                take_sum(nxt)
            cap_and_weigh(s)
            round_page(s)
            if t == planes_in[b] - 1:
                weave(x_planes[b], x_grouped[b], planes_in[b], PJ)
                weave(page_planes[b], page_grouped[b], planes_in[b], T2)
            if s == PACK + 1:
                quantise_x(0)
                quantise_page(0, 0, T2)

        scores = [psum.tile([P, PJ], F32, name=f"scores{m}", tag=f"bank{(m + PACK) % NM}") for m in range(NM)]

        def pass_scores(m, b):
            nc.tensor.matmul_mx(
                out=scores[m][:],
                lhsT=page_codes[b][:, P * m : P * (m + 1)].bitcast(FP8X4),
                lhsT_scale=page_scales[b][:, P * m : P * (m + 1)],
                rhs=x_codes[b][:].bitcast(FP8X4),
                rhs_scale=x_scales[b][:],
                start=(b == 0),
                stop=(b == NB - 1),
            )

        for m in range(NM):
            pass_scores(m, 0)
        quantise_x(1)
        staged = [keep.tile([P, PACK, PJ], F32, name=f"staged{n}", tag=f"big{n}", align_bytes=64) for n in range(2)]
        for m in range(NM):
            if (P * m) % PIECE == 0:
                quantise_page(1, P * m, PIECE)
            pass_scores(m, 1)
            row = staged[m // PACK][:, m % PACK, :]
            nc.vector.tensor_scalar(row, scores[m][:], slot_t[:, m : m + 1], None, ALU.max)
            nc.scalar.activation(out=row, in_=row, func=ACT.Ln)
            nc.sync.dma_start(out=out[P * m : P * (m + 1), :], in_=row)
